import numpy as np
import ml_dtypes


def mxq(x, axis, fmt="e4m3"):
    dtype, down = {"e4m3": (ml_dtypes.float8_e4m3fn, 7), "e5m2": (ml_dtypes.float8_e5m2, 14)}[fmt]
    v = np.moveaxis(np.asarray(x, np.float32).astype(ml_dtypes.bfloat16).astype(np.float64), axis, -1)
    blocks = v.reshape(v.shape[:-1] + (-1, 32))
    amax = np.abs(blocks).max(-1, keepdims=True)
    byte = np.maximum(np.where(amax > 0, np.frexp(amax)[1] - 1 + 127, 0) - down, 1)
    scale = np.exp2(byte - 127.0)
    codes = (blocks / scale).astype(np.float32).astype(dtype).astype(np.float64)
    return np.moveaxis((codes * scale).reshape(v.shape), -1, axis)


WIDE = False


def mx_kscale(k):
    if not WIDE:
        return np.ones(k)
    levels = np.array([10, -10, 5, -5, 0])
    if k % 512:
        return np.exp2(np.random.permutation(np.resize(levels, k // 32))).repeat(32)
    a = np.empty((k // 512, 16))
    for p in range(k // 512):
        a[p, :8] = np.random.permutation(np.resize(levels, 8))
        for g in range(8):
            far = levels[np.abs(levels - a[p, g]) >= 10]
            a[p, g + 8] = far[np.random.randint(len(far))]
    return np.exp2(a.ravel()).repeat(32)


def f64(x):
    return np.asarray(x).astype(np.float64)


def striped8(idx):
    return np.asarray(idx).reshape(8, -1, 16).transpose(0, 2, 1).reshape(128, -1).astype(np.uint16)


def unstriped8(offs):
    return offs.reshape(8, 16, -1).transpose(0, 2, 1).reshape(8, -1).astype(np.int64)


def pick8(x, idx, run):
    r = np.arange(len(x))
    return x[r[:, None], idx[r % (8 * run) // run]]


E2M1 = np.array([0.0, 0.5, 1.0, 1.5, 2.0, 3.0, 4.0, 6.0, -0.0, -0.5, -1.0, -1.5, -2.0, -3.0, -4.0, -6.0])


def pack_weight(w, fmt):
    k, n = w.shape
    w = f64(np.asarray(w, np.float32).astype(ml_dtypes.bfloat16)).reshape(k // 32, 32, n)
    amax = np.abs(w).max(1)
    if fmt == "e4m3":
        byte = np.frexp(amax)[1] - 1 + 127 - 7
    else:
        mant, ex = np.frexp(amax / 6.0)
        byte = np.where(mant > 0.5, ex, ex - 1) + 127
    byte = np.clip(np.where(amax > 0, byte, 1), 1, 254)
    scaled = (w * np.exp2(127.0 - byte)[:, None, :]).reshape(k, n).astype(np.float32)
    by_word = np.ascontiguousarray(scaled.reshape(k // 512, 128, 4, n).transpose(0, 1, 3, 2))
    if fmt == "e4m3":
        words = by_word.astype(ml_dtypes.float8_e4m3fn).view(np.uint8)
    else:
        c = by_word.astype(ml_dtypes.float4_e2m1fn).view(np.uint8) & 0xF
        words = (c[..., 0::2] | (c[..., 1::2] << 4)).reshape(k // 512, 128, 2 * n)
    return np.ascontiguousarray(words), np.ascontiguousarray(byte.astype(np.uint8).reshape(k // 512, 16, n))


def unpack_weight(words, scales, fmt):
    g, _, n = scales.shape
    words = np.ascontiguousarray(words).reshape(g, 128, n, -1)
    if fmt == "e4m3":
        vals = words.view(ml_dtypes.float8_e4m3fn).astype(np.float64)
    else:
        nib = np.empty((g, 128, n, 4), np.uint8)
        nib[..., 0::2] = words & 0xF
        nib[..., 1::2] = words >> 4
        vals = E2M1[nib]
    vals = vals * np.repeat(np.exp2(scales.astype(np.float64) - 127.0), 8, axis=1)[..., None]
    return vals.transpose(0, 1, 3, 2).reshape(g * 512, n)


K, T, J, N = 512, 1024, 512, 512


def setup_inputs():
    n = np.random.standard_normal
    idx = np.stack([np.random.permutation(T)[:J] for _ in range(8)])
    fj = mx_kscale(J)
    tgp = pack_weight(n((J, N)) * fj[:, None], "e4m3")
    return {
        "xf": (n((K, T))).astype(np.float32),
        "rw": (np.random.uniform(0.5, 2.0, (1, J)) / fj).astype(np.float32),
        "tg_words": tgp[0],
        "tg_scales": tgp[1],
        "old": (1.0 * n((K, N))).astype(np.float32),
        "offs": striped8(idx),
    }


def reference(xf, rw, tg_words, tg_scales, old, offs):
    idx = unstriped8(offs)
    tgu = unpack_weight(tg_words, tg_scales, "e4m3")
    xs = pick8(f64(xf), idx, 64) * f64(rw)
    xj = xs.T
    xjq = mxq(xj, 0, "e4m3")
    w = xjq.T @ tgu
    y = 0.04 * w + 0.5 * f64(old)
    return y

@@ -1,0 +1,119 @@
+from contextlib import ExitStack
+
+import concourse.mybir as mybir
+from concourse.masks import make_identity
+
+K, T, J, N = 512, 1024, 512, 512
+FLOPS = 2 * K * J * N
+
+F32 = mybir.dt.float32
+BF16 = mybir.dt.bfloat16
+I32 = mybir.dt.int32
+U32 = mybir.dt.uint32
+U16 = mybir.dt.uint16
+U8 = mybir.dt.uint8
+FP8X4 = mybir.dt.float8_e4m3fn_x4
+MULT = mybir.AluOpType.mult
+ADD = mybir.AluOpType.add
+COPY = mybir.ActivationFunctionType.Copy
+
+P = 128
+PACK = 4
+TILES = K // P
+
+
+def tile_list_head_tokens_to_weights_kernel(tc, xf, rw, tg_words, tg_scales, old, offs, out):
+    nc = tc.nc
+    xf_rows = xf.rearrange("(p a) t -> p a t", a=TILES)
+    old_rows = old.rearrange("(p a) n -> p a n", a=TILES)
+    out_rows = out.rearrange("(p a) n -> p a n", a=TILES)
+
+    with ExitStack() as ctx:
+        keep = ctx.enter_context(tc.tile_pool(name="keep", bufs=1))
+        psum = ctx.enter_context(tc.psum_pool(name="psum", bufs=1))
+
+        offsets = keep.tile([P, J // 16], U16, name="offsets")
+        rw_dealt = keep.tile([P, PACK], F32, name="rw_dealt")
+        windows = [keep.tile([P, T], F32, name="window%d" % a) for a in range(TILES)]
+        tg_codes = keep.tile([P, N], U32, name="tg_codes", align_bytes=64)
+        tg_plane = keep.tile([P, N], U8, name="tg_plane", align_bytes=64)
+        olds = [keep.tile([P, N], F32, name="old%d" % a) for a in range(TILES)]
+        ident = keep.tile([P, P], F32, name="ident")
+
+        nc.vector.memset(tg_plane[:].bitcast(U32), 0)
+        nc.scalar.dma_start(out=rw_dealt[:], in_=rw.rearrange("o (p t) -> (o p) t", t=PACK))
+        nc.sync.dma_start(offsets[:], offs)
+        for q in range(4):
+            nc.scalar.dma_start(
+                out=tg_plane[32 * q : 32 * q + 4, :].bitcast(I32),
+                in_=tg_scales[0][4 * q : 4 * q + 4, :].bitcast(I32),
+            )
+        for a in range(TILES - 1):
+            nc.sync.dma_start(out=windows[a][:], in_=xf_rows[:, a, :])
+        nc.sync.dma_start(out=olds[0][:], in_=old_rows[:, 0, :])
+        nc.sync.dma_start(out=windows[TILES - 1][:], in_=xf_rows[:, TILES - 1, :])
+        nc.sync.dma_start(out=tg_codes[:].bitcast(I32), in_=tg_words[0].rearrange("p n t -> p (n t)").bitcast(I32))
+        for a in range(1, TILES):
+            nc.sync.dma_start(out=olds[a][:], in_=old_rows[:, a, :])
+        make_identity(nc, ident[:])
+
+        rw_bank = psum.tile([P, PACK, P], F32, name="rw_bank")
+        for t in range(PACK):
+            nc.tensor.transpose(rw_bank[:, t, :], rw_dealt[:, t : t + 1].to_broadcast([P, P]), ident[:])
+        rw_all = keep.tile([P, J], F32, name="rw_all")
+        nc.vector.tensor_copy(
+            out=rw_all[:].rearrange("p (q t) -> p q t", t=PACK), in_=rw_bank[:].rearrange("p t q -> p q t")
+        )
+
+        xs = [keep.tile([P, J], F32, name="xs%d" % a) for a in range(TILES)]
+        pairs = [keep.tile([P, J], BF16, name="pairs%d" % a) for a in range(TILES)]
+        grouped = [keep.tile([P, P, PACK], BF16, name="grouped%d" % a, align_bytes=64) for a in range(TILES)]
+        codes = [keep.tile([P, P], U32, name="codes%d" % a, align_bytes=64) for a in range(TILES)]
+        planes = [keep.tile([P, P], U8, name="plane%d" % a, align_bytes=64) for a in range(TILES)]
+        halves = [keep.tile([P, N], F32, name="half%d" % a) for a in range(TILES)]
+        results = [keep.tile([P, N], F32, name="result%d" % a) for a in range(TILES)]
+        accs = [psum.tile([P, N], F32, name="acc%d" % a) for a in range(TILES)]
+
+        def gather(a):
+            nc.vector.tensor_tensor(xs[a][:], windows[a][:].indirect(offsets[:]), rw_all[:], MULT)
+
+        def turn(a):
+            nc.scalar.copy(
+                out=pairs[a][:].rearrange("p (u q e) -> p u q e", u=2, e=2),
+                in_=xs[a][:].rearrange("p (q u e) -> p u q e", u=2, e=2),
+            )
+            words = pairs[a][:].bitcast(F32)
+            turned = psum.tile([P, 2, P], F32, name="turned", bufs=3)
+            for u in range(2):
+                nc.tensor.transpose(turned[:, u, :], words[:, u * P : (u + 1) * P], ident[:])
+            nc.scalar.copy(out=grouped[a][:].bitcast(F32), in_=turned[:].rearrange("q u m -> q m u"))
+
+        def multiply(a):
+            nc.vector.quantize_mx(
+                out=codes[a][:].bitcast(FP8X4), scales=planes[a][:], in_=grouped[a][:].rearrange("q m t -> q (m t)")
+            )
+            nc.tensor.matmul_mx(
+                out=accs[a][:],
+                lhsT=codes[a][:].bitcast(FP8X4),
+                lhsT_scale=planes[a][:],
+                rhs=tg_codes[:].bitcast(FP8X4),
+                rhs_scale=tg_plane[:],
+                start=True,
+                stop=True,
+            )
+
+        def finish(a):
+            nc.scalar.activation(out=halves[a][:], in_=olds[a][:], func=COPY, scale=0.5)
+            nc.vector.scalar_tensor_tensor(
+                out=results[a][:], in0=accs[a][:], scalar=0.04, in1=halves[a][:], op0=MULT, op1=ADD
+            )
+            nc.sync.dma_start(out=out_rows[:, a, :], in_=results[a][:])
+
+        for a in range(TILES):
+            gather(a)
+            turn(a)
+            if a >= 1:
+                multiply(a - 1)
+        multiply(TILES - 1)
+        for a in range(TILES):
+            finish(a)

@@ -20,6 +20,8 @@ COPY = mybir.ActivationFunctionType.Copy
 P = 128
 PACK = 4
 TILES = K // P
+HALF = J // 2
+SPLIT = 320
 
 
 def tile_list_head_tokens_to_weights_kernel(tc, xf, rw, tg_words, tg_scales, old, offs, out):
@@ -37,10 +39,11 @@ def tile_list_head_tokens_to_weights_kernel(tc, xf, rw, tg_words, tg_scales, old
         windows = [keep.tile([P, T], F32, name="window%d" % a) for a in range(TILES)]
         tg_codes = keep.tile([P, N], U32, name="tg_codes", align_bytes=64)
         tg_plane = keep.tile([P, N], U8, name="tg_plane", align_bytes=64)
-        olds = [keep.tile([P, N], F32, name="old%d" % a) for a in range(TILES)]
+        old_early = keep.tile([P, 2, N], F32, name="old_early")
+        old_late = [keep.tile([P, N], F32, name="old_late%d" % a) for a in range(2)]
         ident = keep.tile([P, P], F32, name="ident")
 
-        nc.vector.memset(tg_plane[:].bitcast(U32), 0)
+        nc.gpsimd.memset(tg_plane[:].bitcast(U32), 0)
         nc.scalar.dma_start(out=rw_dealt[:], in_=rw.rearrange("o (p t) -> (o p) t", t=PACK))
         nc.sync.dma_start(offsets[:], offs)
         for q in range(4):
@@ -48,72 +51,110 @@ def tile_list_head_tokens_to_weights_kernel(tc, xf, rw, tg_words, tg_scales, old
                 out=tg_plane[32 * q : 32 * q + 4, :].bitcast(I32),
                 in_=tg_scales[0][4 * q : 4 * q + 4, :].bitcast(I32),
             )
-        for a in range(TILES - 1):
+        for a in range(TILES):
             nc.sync.dma_start(out=windows[a][:], in_=xf_rows[:, a, :])
-        nc.sync.dma_start(out=olds[0][:], in_=old_rows[:, 0, :])
-        nc.sync.dma_start(out=windows[TILES - 1][:], in_=xf_rows[:, TILES - 1, :])
         nc.sync.dma_start(out=tg_codes[:].bitcast(I32), in_=tg_words[0].rearrange("p n t -> p (n t)").bitcast(I32))
-        for a in range(1, TILES):
-            nc.sync.dma_start(out=olds[a][:], in_=old_rows[:, a, :])
+        nc.sync.dma_start(out=old_early[:], in_=old_rows[:, 0:2, :])
+        for a in range(2):
+            nc.sync.dma_start(out=old_late[a][:], in_=old_rows[:, 2 + a, :])
         make_identity(nc, ident[:])
 
-        rw_bank = psum.tile([P, PACK, P], F32, name="rw_bank")
+        rw_bank = psum.tile([P, PACK, P], F32, name="rw_bank", tag="rw_bank")
         for t in range(PACK):
             nc.tensor.transpose(rw_bank[:, t, :], rw_dealt[:, t : t + 1].to_broadcast([P, P]), ident[:])
         rw_all = keep.tile([P, J], F32, name="rw_all")
-        nc.vector.tensor_copy(
-            out=rw_all[:].rearrange("p (q t) -> p q t", t=PACK), in_=rw_bank[:].rearrange("p t q -> p q t")
-        )
+        for h in range(2):
+            nc.scalar.copy(
+                out=rw_all[:, h * HALF : (h + 1) * HALF].rearrange("p (q t) -> p q t", t=PACK),
+                in_=rw_bank[:, :, h * P // 2 : (h + 1) * P // 2].rearrange("p t q -> p q t"),
+            )
 
-        xs = [keep.tile([P, J], F32, name="xs%d" % a) for a in range(TILES)]
-        pairs = [keep.tile([P, J], BF16, name="pairs%d" % a) for a in range(TILES)]
-        grouped = [keep.tile([P, P, PACK], BF16, name="grouped%d" % a, align_bytes=64) for a in range(TILES)]
-        codes = [keep.tile([P, P], U32, name="codes%d" % a, align_bytes=64) for a in range(TILES)]
+        xs = [keep.tile([P, J], F32, name="xs%d" % a, tag="xs%d" % a, align_bytes=64) for a in range(TILES)]
+        stages = [keep.tile([P, N], F32, name="stage%d" % a) for a in range(2)]
+        half_early = keep.tile([P, 2 * N], F32, name="half_early", align_bytes=64)
+        grouped = [half_early[:, 0 : J // 2]] + [
+            keep.tile([P, J // 2], F32, name="grouped%d" % a, align_bytes=64)[:] for a in range(1, TILES)
+        ]
+        code_tags = ["xs2", "xs3", "codes2", "codes3"]
         planes = [keep.tile([P, P], U8, name="plane%d" % a, align_bytes=64) for a in range(TILES)]
-        halves = [keep.tile([P, N], F32, name="half%d" % a) for a in range(TILES)]
+        halves = [half_early[:, 0:N], half_early[:, N : 2 * N], stages[0][:], stages[1][:]]
         results = [keep.tile([P, N], F32, name="result%d" % a) for a in range(TILES)]
-        accs = [psum.tile([P, N], F32, name="acc%d" % a) for a in range(TILES)]
+        turned = [psum.tile([P, 2, P], F32, name="turned%d" % a) for a in range(3)]
+        accs = [psum.tile([P, N], F32, name="acc%d" % a) for a in range(3)]
 
-        def gather(a):
-            nc.vector.tensor_tensor(xs[a][:], windows[a][:].indirect(offsets[:]), rw_all[:], MULT)
+        def gather(a, j0, j1):
+            picked = windows[a][:].indirect(offsets[:, j0 // 16 : j1 // 16])
+            nc.vector.tensor_tensor(xs[a][:, j0:j1], picked, rw_all[:, j0:j1], MULT)
+
+        def cast(a, j0, j1):
+            pairs = stages[a % 2][:, 0 : J // 2].bitcast(BF16).rearrange("p (u q e) -> p u q e", u=2, e=2)
+            nc.scalar.copy(
+                out=pairs[:, :, j0 // PACK : j1 // PACK, :],
+                in_=xs[a][:, j0:j1].rearrange("p (q u e) -> p u q e", u=2, e=2),
+            )
 
         def turn(a):
-            nc.scalar.copy(
-                out=pairs[a][:].rearrange("p (u q e) -> p u q e", u=2, e=2),
-                in_=xs[a][:].rearrange("p (q u e) -> p u q e", u=2, e=2),
-            )
-            words = pairs[a][:].bitcast(F32)
-            turned = psum.tile([P, 2, P], F32, name="turned", bufs=3)
             for u in range(2):
-                nc.tensor.transpose(turned[:, u, :], words[:, u * P : (u + 1) * P], ident[:])
-            nc.scalar.copy(out=grouped[a][:].bitcast(F32), in_=turned[:].rearrange("q u m -> q m u"))
+                nc.tensor.transpose(turned[a % 3][:, u, :], stages[a % 2][:, u * P : (u + 1) * P], ident[:])
 
-        def multiply(a):
-            nc.vector.quantize_mx(
-                out=codes[a][:].bitcast(FP8X4), scales=planes[a][:], in_=grouped[a][:].rearrange("q m t -> q (m t)")
+        def weave(a):
+            nc.scalar.copy(
+                out=grouped[a].rearrange("q (m u) -> q m u", u=2), in_=turned[a % 3][:].rearrange("q u m -> q m u")
             )
+
+        def quantize(a):
+            codes = keep.tile([P, P], U32, name="codes%d" % a, tag=code_tags[a], align_bytes=64)
+            nc.vector.quantize_mx(out=codes[:].bitcast(FP8X4), scales=planes[a][:], in_=grouped[a].bitcast(BF16))
+            return codes
+
+        def multiply(a, codes, acc, n0, n1):
             nc.tensor.matmul_mx(
-                out=accs[a][:],
-                lhsT=codes[a][:].bitcast(FP8X4),
+                out=acc,
+                lhsT=codes[:].bitcast(FP8X4),
                 lhsT_scale=planes[a][:],
-                rhs=tg_codes[:].bitcast(FP8X4),
-                rhs_scale=tg_plane[:],
+                rhs=tg_codes[:, n0:n1].bitcast(FP8X4),
+                rhs_scale=tg_plane[:, n0:n1],
                 start=True,
                 stop=True,
             )
 
-        def finish(a):
-            nc.scalar.activation(out=halves[a][:], in_=olds[a][:], func=COPY, scale=0.5)
-            nc.vector.scalar_tensor_tensor(
-                out=results[a][:], in0=accs[a][:], scalar=0.04, in1=halves[a][:], op0=MULT, op1=ADD
-            )
-            nc.sync.dma_start(out=out_rows[:, a, :], in_=results[a][:])
+        def halve_late(a):
+            nc.scalar.activation(out=halves[a], in_=old_late[a - 2][:], func=COPY, scale=0.5)
 
-        for a in range(TILES):
-            gather(a)
-            turn(a)
+        def finish(a, acc, n0, n1):
+            nc.vector.scalar_tensor_tensor(
+                out=results[a][:, n0:n1], in0=acc, scalar=0.04, in1=halves[a][:, n0:n1], op0=MULT, op1=ADD
+            )
+            nc.sync.dma_start(out=out_rows[:, a, n0:n1], in_=results[a][:, n0:n1])
+
+        gather(0, 0, HALF)
+        gather(0, HALF, J)
+        gather(1, 0, J)
+        gather(2, 0, J)
+        gather(3, 0, SPLIT)
+        gather(3, SPLIT, J)
+        for a in range(3):
+            cast(a, 0, J)
             if a >= 1:
-                multiply(a - 1)
-        multiply(TILES - 1)
-        for a in range(TILES):
-            finish(a)
+                weave(a - 1)
+            turn(a)
+        multiply(0, quantize(0), accs[0][:], 0, N)
+        nc.vector.tensor_scalar_mul(half_early[:], old_early[:].rearrange("p a n -> p (a n)"), 0.5)
+        cast(3, 0, SPLIT)
+        cast(3, SPLIT, J)
+        weave(2)
+        halve_late(2)
+        turn(3)
+        weave(3)
+        halve_late(3)
+        for a in (1, 2):
+            multiply(a, quantize(a), accs[a][:], 0, N)
+        finish(0, accs[0][:], 0, N)
+        last_codes = quantize(3)
+        last_accs = [psum.tile([P, N // 2], F32, name="last_acc%d" % h, tag=tag) for h, tag in enumerate(("last", "rw_bank"))]
+        for h in range(2):
+            multiply(3, last_codes, last_accs[h][:], h * N // 2, (h + 1) * N // 2)
+        for a in (1, 2):
+            finish(a, accs[a][:], 0, N)
+        for h in range(2):
+            finish(3, last_accs[h][:], h * N // 2, (h + 1) * N // 2)

@@ -35,7 +35,7 @@ def tile_list_head_tokens_to_weights_kernel(tc, xf, rw, tg_words, tg_scales, old
         psum = ctx.enter_context(tc.psum_pool(name="psum", bufs=1))
 
         offsets = keep.tile([P, J // 16], U16, name="offsets")
-        rw_dealt = keep.tile([P, PACK], F32, name="rw_dealt")
+        rw_dealt = [keep.tile([P, 2], F32, name="rw_dealt%d" % h) for h in range(2)]
         windows = [keep.tile([P, T], F32, name="window%d" % a) for a in range(TILES)]
         tg_codes = keep.tile([P, N], U32, name="tg_codes", align_bytes=64)
         tg_plane = keep.tile([P, N], U8, name="tg_plane", align_bytes=64)
@@ -44,10 +44,13 @@ def tile_list_head_tokens_to_weights_kernel(tc, xf, rw, tg_words, tg_scales, old
         ident = keep.tile([P, P], F32, name="ident")
 
         nc.gpsimd.memset(tg_plane[:].bitcast(U32), 0)
-        nc.scalar.dma_start(out=rw_dealt[:], in_=rw.rearrange("o (p t) -> (o p) t", t=PACK))
+        for h in range(2):
+            nc.scalar.dma_start(
+                out=rw_dealt[h][:], in_=rw[:, h * HALF : (h + 1) * HALF].rearrange("o (p e) -> (o p) e", e=2)
+            )
         nc.sync.dma_start(offsets[:], offs)
         for q in range(4):
-            nc.scalar.dma_start(
+            nc.sync.dma_start(
                 out=tg_plane[32 * q : 32 * q + 4, :].bitcast(I32),
                 in_=tg_scales[0][4 * q : 4 * q + 4, :].bitcast(I32),
             )
@@ -59,14 +62,14 @@ def tile_list_head_tokens_to_weights_kernel(tc, xf, rw, tg_words, tg_scales, old
             nc.sync.dma_start(out=old_late[a][:], in_=old_rows[:, 2 + a, :])
         make_identity(nc, ident[:])
 
-        rw_bank = psum.tile([P, PACK, P], F32, name="rw_bank", tag="rw_bank")
-        for t in range(PACK):
-            nc.tensor.transpose(rw_bank[:, t, :], rw_dealt[:, t : t + 1].to_broadcast([P, P]), ident[:])
         rw_all = keep.tile([P, J], F32, name="rw_all")
         for h in range(2):
+            rw_bank = psum.tile([P, 2, P], F32, name="rw_bank%d" % h, tag="edge%d" % h)
+            for e in range(2):
+                nc.tensor.transpose(rw_bank[:, e, :], rw_dealt[h][:, e : e + 1].to_broadcast([P, P]), ident[:])
             nc.scalar.copy(
-                out=rw_all[:, h * HALF : (h + 1) * HALF].rearrange("p (q t) -> p q t", t=PACK),
-                in_=rw_bank[:, :, h * P // 2 : (h + 1) * P // 2].rearrange("p t q -> p q t"),
+                out=rw_all[:, h * HALF : (h + 1) * HALF].rearrange("p (q e) -> p q e", e=2),
+                in_=rw_bank[:].rearrange("p e q -> p q e"),
             )
 
         xs = [keep.tile([P, J], F32, name="xs%d" % a, tag="xs%d" % a, align_bytes=64) for a in range(TILES)]
@@ -151,7 +154,7 @@ def tile_list_head_tokens_to_weights_kernel(tc, xf, rw, tg_words, tg_scales, old
             multiply(a, quantize(a), accs[a][:], 0, N)
         finish(0, accs[0][:], 0, N)
         last_codes = quantize(3)
-        last_accs = [psum.tile([P, N // 2], F32, name="last_acc%d" % h, tag=tag) for h, tag in enumerate(("last", "rw_bank"))]
+        last_accs = [psum.tile([P, N // 2], F32, name="last_acc%d" % h, tag="edge%d" % h) for h in range(2)]
         for h in range(2):
             multiply(3, last_codes, last_accs[h][:], h * N // 2, (h + 1) * N // 2)
         for a in (1, 2):

@@ -35,7 +35,7 @@ def tile_list_head_tokens_to_weights_kernel(tc, xf, rw, tg_words, tg_scales, old
         psum = ctx.enter_context(tc.psum_pool(name="psum", bufs=1))
 
         offsets = keep.tile([P, J // 16], U16, name="offsets")
-        rw_dealt = [keep.tile([P, 2], F32, name="rw_dealt%d" % h) for h in range(2)]
+        rw_dealt = keep.tile([P, 2, 2], F32, name="rw_dealt")
         windows = [keep.tile([P, T], F32, name="window%d" % a) for a in range(TILES)]
         tg_codes = keep.tile([P, N], U32, name="tg_codes", align_bytes=64)
         tg_plane = keep.tile([P, N], U8, name="tg_plane", align_bytes=64)
@@ -44,19 +44,16 @@ def tile_list_head_tokens_to_weights_kernel(tc, xf, rw, tg_words, tg_scales, old
         ident = keep.tile([P, P], F32, name="ident")
 
         nc.gpsimd.memset(tg_plane[:].bitcast(U32), 0)
-        for h in range(2):
-            nc.scalar.dma_start(
-                out=rw_dealt[h][:], in_=rw[:, h * HALF : (h + 1) * HALF].rearrange("o (p e) -> (o p) e", e=2)
-            )
+        nc.scalar.dma_start(out=rw_dealt[:], in_=rw.rearrange("o (h p e) -> p (o h) e", h=2, e=2))
         nc.sync.dma_start(offsets[:], offs)
+        for a in range(TILES):
+            nc.sync.dma_start(out=windows[a][:], in_=xf_rows[:, a, :])
+        nc.sync.dma_start(out=tg_codes[:].bitcast(I32), in_=tg_words[0].rearrange("p n t -> p (n t)").bitcast(I32))
         for q in range(4):
             nc.sync.dma_start(
                 out=tg_plane[32 * q : 32 * q + 4, :].bitcast(I32),
                 in_=tg_scales[0][4 * q : 4 * q + 4, :].bitcast(I32),
             )
-        for a in range(TILES):
-            nc.sync.dma_start(out=windows[a][:], in_=xf_rows[:, a, :])
-        nc.sync.dma_start(out=tg_codes[:].bitcast(I32), in_=tg_words[0].rearrange("p n t -> p (n t)").bitcast(I32))
         nc.sync.dma_start(out=old_early[:], in_=old_rows[:, 0:2, :])
         for a in range(2):
             nc.sync.dma_start(out=old_late[a][:], in_=old_rows[:, 2 + a, :])
@@ -66,7 +63,7 @@ def tile_list_head_tokens_to_weights_kernel(tc, xf, rw, tg_words, tg_scales, old
         for h in range(2):
             rw_bank = psum.tile([P, 2, P], F32, name="rw_bank%d" % h, tag="edge%d" % h)
             for e in range(2):
-                nc.tensor.transpose(rw_bank[:, e, :], rw_dealt[h][:, e : e + 1].to_broadcast([P, P]), ident[:])
+                nc.tensor.transpose(rw_bank[:, e, :], rw_dealt[:, h, e : e + 1].to_broadcast([P, P]), ident[:])
             nc.scalar.copy(
                 out=rw_all[:, h * HALF : (h + 1) * HALF].rearrange("p (q e) -> p q e", e=2),
                 in_=rw_bank[:].rearrange("p e q -> p q e"),

from contextlib import ExitStack

import concourse.mybir as mybir
from concourse.masks import make_identity

K, T, J, N = 512, 1024, 512, 512
FLOPS = 2 * K * J * N

F32 = mybir.dt.float32
BF16 = mybir.dt.bfloat16
I32 = mybir.dt.int32
U32 = mybir.dt.uint32
U16 = mybir.dt.uint16
U8 = mybir.dt.uint8
FP8X4 = mybir.dt.float8_e4m3fn_x4
MULT = mybir.AluOpType.mult
ADD = mybir.AluOpType.add
COPY = mybir.ActivationFunctionType.Copy

P = 128
PACK = 4
TILES = K // P
HALF = J // 2
SPLIT = 320


def tile_list_head_tokens_to_weights_kernel(tc, xf, rw, tg_words, tg_scales, old, offs, out):
    nc = tc.nc
    xf_rows = xf.rearrange("(p a) t -> p a t", a=TILES)
    old_rows = old.rearrange("(p a) n -> p a n", a=TILES)
    out_rows = out.rearrange("(p a) n -> p a n", a=TILES)

    with ExitStack() as ctx:
        keep = ctx.enter_context(tc.tile_pool(name="keep", bufs=1))
        psum = ctx.enter_context(tc.psum_pool(name="psum", bufs=1))

        offsets = keep.tile([P, J // 16], U16, name="offsets")
        rw_dealt = keep.tile([P, 2, 2], F32, name="rw_dealt")
        windows = [keep.tile([P, T], F32, name="window%d" % a) for a in range(TILES)]
        tg_codes = keep.tile([P, N], U32, name="tg_codes", align_bytes=64)
        tg_plane = keep.tile([P, N], U8, name="tg_plane", align_bytes=64)
        old_early = keep.tile([P, 2, N], F32, name="old_early")
        old_late = [keep.tile([P, N], F32, name="old_late%d" % a) for a in range(2)]
        ident = keep.tile([P, P], F32, name="ident")

        nc.gpsimd.memset(tg_plane[:].bitcast(U32), 0)
        nc.scalar.dma_start(out=rw_dealt[:], in_=rw.rearrange("o (h p e) -> p (o h) e", h=2, e=2))
        nc.sync.dma_start(offsets[:], offs)
        for a in range(TILES):
            nc.sync.dma_start(out=windows[a][:], in_=xf_rows[:, a, :])
        nc.sync.dma_start(out=tg_codes[:].bitcast(I32), in_=tg_words[0].rearrange("p n t -> p (n t)").bitcast(I32))
        for q in range(4):
            nc.sync.dma_start(
                out=tg_plane[32 * q : 32 * q + 4, :].bitcast(I32),
                in_=tg_scales[0][4 * q : 4 * q + 4, :].bitcast(I32),
            )
        nc.sync.dma_start(out=old_early[:], in_=old_rows[:, 0:2, :])
        for a in range(2):
            nc.sync.dma_start(out=old_late[a][:], in_=old_rows[:, 2 + a, :])
        make_identity(nc, ident[:])

        rw_all = keep.tile([P, J], F32, name="rw_all")
        for h in range(2):
            rw_bank = psum.tile([P, 2, P], F32, name="rw_bank%d" % h, tag="edge%d" % h)
            for e in range(2):
                nc.tensor.transpose(rw_bank[:, e, :], rw_dealt[:, h, e : e + 1].to_broadcast([P, P]), ident[:])
            nc.scalar.copy(
                out=rw_all[:, h * HALF : (h + 1) * HALF].rearrange("p (q e) -> p q e", e=2),
                in_=rw_bank[:].rearrange("p e q -> p q e"),
            )

        xs = [keep.tile([P, J], F32, name="xs%d" % a, tag="xs%d" % a, align_bytes=64) for a in range(TILES)]
        stages = [keep.tile([P, N], F32, name="stage%d" % a) for a in range(2)]
        half_early = keep.tile([P, 2 * N], F32, name="half_early", align_bytes=64)
        grouped = [half_early[:, 0 : J // 2]] + [
            keep.tile([P, J // 2], F32, name="grouped%d" % a, align_bytes=64)[:] for a in range(1, TILES)
        ]
        code_tags = ["xs2", "xs3", "codes2", "codes3"]
        planes = [keep.tile([P, P], U8, name="plane%d" % a, align_bytes=64) for a in range(TILES)]
        halves = [half_early[:, 0:N], half_early[:, N : 2 * N], stages[0][:], stages[1][:]]
        results = [keep.tile([P, N], F32, name="result%d" % a) for a in range(TILES)]
        turned = [psum.tile([P, 2, P], F32, name="turned%d" % a) for a in range(3)]
        accs = [psum.tile([P, N], F32, name="acc%d" % a) for a in range(3)]

        def gather(a, j0, j1):
            picked = windows[a][:].indirect(offsets[:, j0 // 16 : j1 // 16])
            nc.vector.tensor_tensor(xs[a][:, j0:j1], picked, rw_all[:, j0:j1], MULT)

        def cast(a, j0, j1):
            pairs = stages[a % 2][:, 0 : J // 2].bitcast(BF16).rearrange("p (u q e) -> p u q e", u=2, e=2)
            nc.scalar.copy(
                out=pairs[:, :, j0 // PACK : j1 // PACK, :],
                in_=xs[a][:, j0:j1].rearrange("p (q u e) -> p u q e", u=2, e=2),
            )

        def turn(a):
            for u in range(2):
                nc.tensor.transpose(turned[a % 3][:, u, :], stages[a % 2][:, u * P : (u + 1) * P], ident[:])

        def weave(a):
            nc.scalar.copy(
                out=grouped[a].rearrange("q (m u) -> q m u", u=2), in_=turned[a % 3][:].rearrange("q u m -> q m u")
            )

        def quantize(a):
            codes = keep.tile([P, P], U32, name="codes%d" % a, tag=code_tags[a], align_bytes=64)
            nc.vector.quantize_mx(out=codes[:].bitcast(FP8X4), scales=planes[a][:], in_=grouped[a].bitcast(BF16))
            return codes

        def multiply(a, codes, acc, n0, n1):
            nc.tensor.matmul_mx(
                out=acc,
                lhsT=codes[:].bitcast(FP8X4),
                lhsT_scale=planes[a][:],
                rhs=tg_codes[:, n0:n1].bitcast(FP8X4),
                rhs_scale=tg_plane[:, n0:n1],
                start=True,
                stop=True,
            )

        def halve_late(a):
            nc.scalar.activation(out=halves[a], in_=old_late[a - 2][:], func=COPY, scale=0.5)

        def finish(a, acc, n0, n1):
            nc.vector.scalar_tensor_tensor(
                out=results[a][:, n0:n1], in0=acc, scalar=0.04, in1=halves[a][:, n0:n1], op0=MULT, op1=ADD
            )
            nc.sync.dma_start(out=out_rows[:, a, n0:n1], in_=results[a][:, n0:n1])

        gather(0, 0, HALF)
        gather(0, HALF, J)
        gather(1, 0, J)
        gather(2, 0, J)
        gather(3, 0, SPLIT)
        gather(3, SPLIT, J)
        for a in range(3):
            cast(a, 0, J)
            if a >= 1:
                weave(a - 1)
            turn(a)
        multiply(0, quantize(0), accs[0][:], 0, N)
        nc.vector.tensor_scalar_mul(half_early[:], old_early[:].rearrange("p a n -> p (a n)"), 0.5)
        cast(3, 0, SPLIT)
        cast(3, SPLIT, J)
        weave(2)
        halve_late(2)
        turn(3)
        weave(3)
        halve_late(3)
        for a in (1, 2):
            multiply(a, quantize(a), accs[a][:], 0, N)
        finish(0, accs[0][:], 0, N)
        last_codes = quantize(3)
        last_accs = [psum.tile([P, N // 2], F32, name="last_acc%d" % h, tag="edge%d" % h) for h in range(2)]
        for h in range(2):
            multiply(3, last_codes, last_accs[h][:], h * N // 2, (h + 1) * N // 2)
        for a in (1, 2):
            finish(a, accs[a][:], 0, N)
        for h in range(2):
            finish(3, last_accs[h][:], h * N // 2, (h + 1) * N // 2)
